import numpy as np
import ml_dtypes


def mxq(x, axis, fmt="e4m3"):
    dtype, down = {"e4m3": (ml_dtypes.float8_e4m3fn, 7), "e5m2": (ml_dtypes.float8_e5m2, 14)}[fmt]
    v = np.moveaxis(np.asarray(x, np.float32).astype(ml_dtypes.bfloat16).astype(np.float64), axis, -1)
    blocks = v.reshape(v.shape[:-1] + (-1, 32))
    amax = np.abs(blocks).max(-1, keepdims=True)
    byte = np.maximum(np.where(amax > 0, np.frexp(amax)[1] - 1 + 127, 0) - down, 1)
    scale = np.exp2(byte - 127.0)
    codes = (blocks / scale).astype(np.float32).astype(dtype).astype(np.float64)
    return np.moveaxis((codes * scale).reshape(v.shape), -1, axis)


WIDE = False


def mx_kscale(k):
    if not WIDE:
        return np.ones(k)
    levels = np.array([10, -10, 5, -5, 0])
    if k % 512:
        return np.exp2(np.random.permutation(np.resize(levels, k // 32))).repeat(32)
    a = np.empty((k // 512, 16))
    for p in range(k // 512):
        a[p, :8] = np.random.permutation(np.resize(levels, 8))
        for g in range(8):
            far = levels[np.abs(levels - a[p, g]) >= 10]
            a[p, g + 8] = far[np.random.randint(len(far))]
    return np.exp2(a.ravel()).repeat(32)


def f64(x):
    return np.asarray(x).astype(np.float64)


def striped(idx):
    return np.tile(idx.reshape(-1, 16).T, (8, 1)).astype(np.uint16)


def unstriped(offs):
    return offs[:16].T.reshape(-1).astype(np.int64)


def striped8(idx):
    return np.concatenate([x.reshape(-1, 16).T for x in idx]).astype(np.uint16)


def runs(offs, k):
    lists = np.stack([offs[16 * r : 16 * r + 16].T.reshape(-1) for r in range(8)]).astype(np.int64)
    return lists[np.arange(k) % 512 // 64]


def pack_weight(w):
    k, n = w.shape
    w = f64(np.asarray(w, np.float32).astype(ml_dtypes.bfloat16)).reshape(k // 32, 32, n)
    amax = np.abs(w).max(1)
    byte = np.clip(np.where(amax > 0, np.frexp(amax)[1] - 1 + 127 - 7, 1), 1, 254)
    scaled = (w * np.exp2(127.0 - byte)[:, None, :]).reshape(k, n).astype(np.float32)
    words = np.ascontiguousarray(scaled.reshape(k // 512, 128, 4, n).transpose(0, 1, 3, 2)).astype(ml_dtypes.float8_e4m3fn).view(np.uint8)
    return words, np.ascontiguousarray(byte.astype(np.uint8).reshape(k // 512, 16, n))


def unpack_weight(words, scales):
    g, p, n, _ = words.shape
    vals = np.ascontiguousarray(words).view(ml_dtypes.float8_e4m3fn).astype(np.float64) * np.repeat(np.exp2(scales.astype(np.float64) - 127.0), 8, axis=1)[..., None]
    return vals.transpose(0, 1, 3, 2).reshape(g * 512, n)


def sigmoid(v):
    return 1.0 / (1.0 + np.exp(-np.maximum(v, -700.0)))


K, T, S, G, H, W, C = 512, 1024, 512, 2048, 512, 384, 512


def setup_inputs():
    n = np.random.standard_normal
    s = mx_kscale(K)[:, None]
    packed_xT = pack_weight(n((K, T)) * s)
    packed_dT = pack_weight(n((K, G)) / s)
    return {
        "x_words": packed_xT[0],
        "x_scales": packed_xT[1],
        "d_words": packed_dT[0],
        "d_scales": packed_dT[1],
        "gs": (np.random.uniform(0.5, 1.5, (K, 1)) / s).astype(np.float32),
        "tau": np.random.uniform(0.3, 0.9, (C, 1)).astype(np.float32),
        "offs": striped(np.random.permutation(T)[:S]),
        "k1": striped8(np.random.randint(0, G, (8, H))),
        "n1": striped(np.random.permutation(S)[:W]),
        "n2": striped(np.random.permutation(S)[:W]),
        "cand": striped(np.random.permutation(T)[:C]),
        "n3": striped(np.random.randint(0, S, G)),
    }


def reference(x_words, x_scales, d_words, d_scales, gs, tau, offs, k1, n1, n2, cand, n3):
    x_cand = unpack_weight(x_words, x_scales)[:, unstriped(cand)]
    d_k1 = unpack_weight(d_words, d_scales)[np.arange(K)[:, None], runs(k1, K)]
    xq = unpack_weight(x_words, x_scales)[:, unstriped(offs)]
    h = 0.0625 * (d_k1.T @ xq)
    old = h[:, unstriped(n1)]
    pa = h[:, unstriped(n2)]
    ra = old * sigmoid(pa)
    ds = h.copy()
    ds[:, unstriped(n1)] = ra
    z = f64(gs) * ds
    s = 0.0625 * ((x_cand.T @ mxq(z, 0, "e4m3")))
    top = s.max(axis=1, keepdims=True)
    ea = np.exp(f64(tau) * (s[:, unstriped(n3)] - top))
    mx = ea.reshape(C, S, 4).max(axis=2)
    mn = ea.reshape(C, S, 4).min(axis=2)
    return 3.0 * (s * (mx - mn))

@@ -1,0 +1,218 @@
+from contextlib import ExitStack
+
+import concourse.mybir as mybir
+
+K, T, S, G, H, W, C = 512, 1024, 512, 2048, 512, 384, 512
+FLOPS = 2 * K * H * S + 2 * H * C * S
+
+F32 = mybir.dt.float32
+BF16 = mybir.dt.bfloat16
+I32 = mybir.dt.int32
+U32 = mybir.dt.uint32
+U16 = mybir.dt.uint16
+U8 = mybir.dt.uint8
+FP8X4 = mybir.dt.float8_e4m3fn_x4
+ALU = mybir.AluOpType
+ACT = mybir.ActivationFunctionType
+
+P = 128
+PACK = 4
+HALF = S // 2
+MEMBERS = 4
+S_WIN = 512
+EXP_N = 256
+
+
+def tile_picked_pqckgateegp_none_p_kernel(
+    tc, x_words, x_scales, d_words, d_scales, gs, tau, offs, k1, n1, n2, cand, n3, out
+):
+    nc = tc.nc
+    with ExitStack() as ctx:
+        keep = ctx.enter_context(tc.tile_pool(name="keep", bufs=1))
+        work = ctx.enter_context(tc.tile_pool(name="work", bufs=2))
+        psum = ctx.enter_context(tc.psum_pool(name="psum", bufs=1))
+
+        def load_list(src, name):
+            tile = keep.tile([P, src.shape[1]], U16, name=name)
+            nc.sync.dma_start(tile[:], src)
+            return tile
+
+        def deal(dst, src, line):
+            nc.vector.tensor_copy(
+                dst.rearrange("p (t b i) -> p b t i", t=PACK, i=line),
+                src.rearrange("p (b i t) -> p b t i", t=PACK, i=line),
+            )
+
+        d_scale_tab = keep.tile([P, G], U8, name="d_scale_tab")
+        x_scale_tab = keep.tile([P, T], U8, name="x_scale_tab")
+        d_plane = keep.tile([P, H], U8, name="d_plane", align_bytes=64)
+        nc.vector.memset(d_scale_tab[:].bitcast(I32), 0)
+        nc.vector.memset(x_scale_tab[:].bitcast(I32), 0)
+        nc.vector.memset(d_plane[:].bitcast(I32), 0)
+
+        k1_t = load_list(k1, "k1_t")
+        nc.sync.dma_start(d_scale_tab[0:P:8, :].bitcast(I32), d_scales[0].bitcast(I32))
+        offs_t = load_list(offs, "offs_t")
+        x_word_tab = keep.tile([P, T], I32, name="x_word_tab")
+        d_word_tab = keep.tile([P, G], I32, name="d_word_tab")
+        nc.sync.dma_start(x_word_tab[:], x_words[0].rearrange("p n t -> p (n t)").bitcast(I32))
+        nc.sync.dma_start(d_word_tab[:], d_words[0].rearrange("p n t -> p (n t)").bitcast(I32))
+        for q in range(4):
+            nc.scalar.dma_start(
+                x_scale_tab[32 * q : 32 * q + 4, :].bitcast(I32), x_scales[0, 4 * q : 4 * q + 4, :].bitcast(I32)
+            )
+        n1_t = load_list(n1, "n1_t")
+        n2_t = load_list(n2, "n2_t")
+        cand_t = load_list(cand, "cand_t")
+        n3_t = load_list(n3, "n3_t")
+        tau_t = keep.tile([P, PACK], F32, name="tau_t")
+        nc.scalar.dma_start(tau_t[:], tau.rearrange("(p b) o -> p (b o)", b=PACK))
+        gs_t = keep.tile([P, PACK], F32, name="gs_t")
+        nc.scalar.dma_start(gs_t[:], gs.rearrange("(p t) o -> p (t o)", t=PACK))
+
+        s_win = [keep.tile([P, S_WIN], F32, name="s_win%d" % b) for b in range(C // P)]
+
+        d_bytes = keep.tile([P, H], U8, name="d_bytes", tag="d_bytes")
+        nc.vector.tensor_copy(d_bytes[:], d_scale_tab[:].indirect(k1_t[:]))
+        d_dealt_bytes = keep.tile([P, H], U8, name="d_dealt_bytes")
+        deal(d_dealt_bytes[:], d_bytes[:], 16)
+        for r in range(4):
+            nc.scalar.dma_start(d_plane[r:P:32, :].bitcast(I32), d_dealt_bytes[8 * r : P : 32, :].bitcast(I32))
+
+        xq_plane = keep.tile([P, S], U8, name="xq_plane", align_bytes=64)
+        nc.vector.tensor_copy(xq_plane[:], x_scale_tab[:].indirect(offs_t[:]))
+        xq_words = keep.tile([P, S], U32, name="xq_words", align_bytes=64)
+        nc.vector.tensor_copy(xq_words[:], x_word_tab[:].bitcast(U32).indirect(offs_t[:]))
+        d_picked = keep.tile([P, H], U32, name="d_picked")
+        nc.vector.tensor_copy(d_picked[:], d_word_tab[:].bitcast(U32).indirect(k1_t[:]))
+        d_dealt = keep.tile([P, H], I32, name="d_dealt", align_bytes=64)
+        deal(d_dealt[:], d_picked[:].bitcast(I32), 4)
+
+        neg_tau = keep.tile([P, C // P], F32, name="neg_tau", tag="d_bytes")
+        nc.scalar.activation(neg_tau[:], tau_t[:], ACT.Copy, scale=-1.0)
+
+        def first_product(bank, t, cols):
+            rows = slice(P * t, P * (t + 1))
+            nc.tensor.matmul_mx(
+                out=bank, lhsT=d_dealt[:, rows].bitcast(FP8X4), lhsT_scale=d_plane[:, rows],
+                rhs=xq_words[:, cols].bitcast(FP8X4), rhs_scale=xq_plane[:, cols], start=True, stop=True,
+            )
+
+        h0_ps = [psum.tile([P, HALF], F32, name="h0_ps%d" % u, tag="bank%d" % u) for u in range(2)]
+        for u in range(2):
+            first_product(h0_ps[u][:], 0, slice(HALF * u, HALF * (u + 1)))
+        h_ps = {}
+        for t in range(1, PACK):
+            h_ps[t] = psum.tile([P, S], F32, name="h_ps%d" % t, tag="bank%d" % (t + 1))
+            first_product(h_ps[t][:], t, slice(0, S))
+
+        h = [keep.tile([P, S], F32, name="h%d" % t) for t in range(PACK)]
+        old = [keep.tile([P, W], F32, name="old%d" % t) for t in range(PACK)]
+        pa = [keep.tile([P, W], F32, name="pa%d" % t) for t in range(PACK)]
+        th = [keep.tile([P, W], F32, name="th%d" % t) for t in range(PACK)]
+        ra = [keep.tile([P, W], F32, name="ra%d" % t) for t in range(PACK)]
+        z = [keep.tile([P, HALF, PACK], BF16, name="z%d" % u, align_bytes=64) for u in range(2)]
+
+        def fetch(t):
+            if t == 0:
+                nc.scalar.activation(h[0][:, :HALF], h0_ps[0][:], ACT.Copy, scale=0.0625)
+                nc.vector.tensor_scalar(h[0][:, HALF:], h0_ps[1][:], 0.0625, None, ALU.mult)
+            else:
+                nc.vector.tensor_scalar(h[t][:], h_ps[t][:], 0.0625, None, ALU.mult)
+            nc.scalar.activation(old[t][:], h[t][:].indirect(n1_t[:]), ACT.Copy, scale=0.5)
+            nc.vector.tensor_copy(pa[t][:], h[t][:].indirect(n2_t[:]))
+            nc.scalar.activation(th[t][:], pa[t][:], ACT.Tanh, scale=0.5)
+            nc.vector.scalar_tensor_tensor(ra[t][:], th[t][:], 1.0, old[t][:], ALU.add, ALU.mult)
+
+        def put(t):
+            nc.scalar.activation(h[t][:].indirect(n1_t[:]), ra[t][:], ACT.Copy)
+            for u in range(2):
+                nc.vector.tensor_scalar(
+                    z[u][:, :, t], h[t][:, HALF * u : HALF * (u + 1)], gs_t[:, t : t + 1], None, ALU.mult
+                )
+
+        fetch(0)
+        fetch(1)
+        put(0)
+        fetch(2)
+        put(1)
+        fetch(3)
+
+        xc_picked = keep.tile([P, C], U32, name="xc_picked")
+        nc.vector.tensor_copy(xc_picked[:], x_word_tab[:].bitcast(U32).indirect(cand_t[:]))
+        xc_bytes = keep.tile([P, C], U8, name="xc_bytes")
+        nc.vector.tensor_copy(xc_bytes[:], x_scale_tab[:].indirect(cand_t[:]))
+        xc_words = keep.tile([P, C], I32, name="xc_words", align_bytes=64)
+        deal(xc_words[:], xc_picked[:].bitcast(I32), 4)
+        xc_plane = keep.tile([P, C], U8, name="xc_plane", align_bytes=64)
+        deal(xc_plane[:], xc_bytes[:], 16)
+
+        put(2)
+        put(3)
+
+        z_words = keep.tile([P, S], U32, name="z_words", align_bytes=64)
+        z_plane = keep.tile([P, S], U8, name="z_plane", align_bytes=64)
+        for u in range(2):
+            cols = slice(HALF * u, HALF * (u + 1))
+            nc.vector.quantize_mx(
+                out=z_words[:, cols].bitcast(FP8X4), scales=z_plane[:, cols],
+                in_=z[u][:].rearrange("p j t -> p (j t)"),
+            )
+
+        def score(bank, b, cols):
+            rows = slice(P * b, P * (b + 1))
+            nc.tensor.matmul_mx(
+                out=bank, lhsT=xc_words[:, rows].bitcast(FP8X4), lhsT_scale=xc_plane[:, rows],
+                rhs=z_words[:, cols].bitcast(FP8X4), rhs_scale=z_plane[:, cols], start=True, stop=True,
+            )
+
+        bias = [keep.tile([P, 1], F32, name="bias%d" % b) for b in range(C // P)]
+        tops = [keep.tile([P, 1], F32, name="top0_%d" % u) for u in range(2)]
+        for u in range(2):
+            cols = slice(HALF * u, HALF * (u + 1))
+            bank = psum.tile([P, HALF], F32, name="s_ps0_%d" % u, tag="bank%d" % (5 + u))
+            score(bank[:], 0, cols)
+            nc.vector.tensor_scalar(
+                s_win[0][:, cols], bank[:], 0.0625, tops[0][:] if u else None, ALU.mult, ALU.max, accum_out=tops[u][:]
+            )
+        nc.scalar.activation(bias[0][:], tops[1][:], ACT.Copy, scale=neg_tau[:, 0:1])
+        for b in range(1, C // P):
+            bank = psum.tile([P, S], F32, name="s_ps%d" % b, tag="bank%d" % ((6 + b) % 8))
+            score(bank[:], b, slice(0, S))
+            top = keep.tile([P, 1], F32, name="top%d" % b)
+            nc.vector.tensor_scalar(s_win[b][:, :S], bank[:], 0.0625, None, ALU.mult, ALU.max, accum_out=top[:])
+            nc.vector.tensor_scalar(bias[b][:], top[:], neg_tau[:, b : b + 1], None, ALU.mult)
+
+        def exps(b, j0, n, hi, lo):
+            ea = work.tile([P, n, MEMBERS], F32, name="ea", tag="ea", bufs=4)
+            flat = ea[:].rearrange("p j m -> p (j m)")
+            for e0 in range(0, n * MEMBERS, EXP_N):
+                c0 = (j0 * MEMBERS + e0) // 16
+                nc.scalar.activation(
+                    flat[:, e0 : e0 + EXP_N], s_win[b][:].indirect(n3_t[:, c0 : c0 + EXP_N // 16]), ACT.Exp,
+                    bias=bias[b][:], scale=tau_t[:, b : b + 1],
+                )
+            nc.vector.tensor_tensor(hi[:, j0 : j0 + n, :], ea[:, :, 0:2], ea[:, :, 2:4], ALU.max)
+            nc.vector.tensor_tensor(lo[:, j0 : j0 + n, :], ea[:, :, 0:2], ea[:, :, 2:4], ALU.min)
+
+        def finish(b, j0, n, hi, lo):
+            cols = slice(j0, j0 + n)
+            mx = work.tile([P, n], F32, name="mx", tag="mx")
+            mn = work.tile([P, n], F32, name="mn", tag="mn")
+            nc.vector.tensor_tensor(mx[:], hi[:, cols, 0], hi[:, cols, 1], ALU.max)
+            nc.vector.tensor_tensor(mn[:], lo[:, cols, 0], lo[:, cols, 1], ALU.min)
+            gap = work.tile([P, n], F32, name="gap", tag="gap")
+            nc.vector.tensor_tensor(gap[:], mx[:], mn[:], ALU.subtract)
+            res = work.tile([P, n], F32, name="res", tag="res", bufs=3)
+            nc.vector.scalar_tensor_tensor(res[:], gap[:], 3.0, s_win[b][:, cols], ALU.mult, ALU.mult)
+            nc.sync.dma_start(out.rearrange("(p b) j -> p b j", b=PACK)[:, b, cols], res[:])
+
+        for b in range(C // P):
+            hi = work.tile([P, S, 2], F32, name="hi", tag="hi")
+            lo = work.tile([P, S, 2], F32, name="lo", tag="lo")
+            j0 = 0
+            for n in ([128, 128, 256] if b == 0 else [256, 256]):
+                exps(b, j0, n, hi, lo)
+                j0 = j0 + n
+                if j0 % HALF == 0:
+                    finish(b, j0 - HALF, HALF, hi, lo)

@@ -19,8 +19,8 @@ P = 128
 PACK = 4
 HALF = S // 2
 MEMBERS = 4
-S_WIN = 512
-EXP_N = 256
+S_WIN = 1024
+EXP_N = 512
 
 
 def tile_picked_pqckgateegp_none_p_kernel(
@@ -53,24 +53,34 @@ def tile_picked_pqckgateegp_none_p_kernel(
         k1_t = load_list(k1, "k1_t")
         nc.sync.dma_start(d_scale_tab[0:P:8, :].bitcast(I32), d_scales[0].bitcast(I32))
         offs_t = load_list(offs, "offs_t")
-        x_word_tab = keep.tile([P, T], I32, name="x_word_tab")
-        d_word_tab = keep.tile([P, G], I32, name="d_word_tab")
-        nc.sync.dma_start(x_word_tab[:], x_words[0].rearrange("p n t -> p (n t)").bitcast(I32))
-        nc.sync.dma_start(d_word_tab[:], d_words[0].rearrange("p n t -> p (n t)").bitcast(I32))
         for q in range(4):
-            nc.scalar.dma_start(
+            nc.sync.dma_start(
                 x_scale_tab[32 * q : 32 * q + 4, :].bitcast(I32), x_scales[0, 4 * q : 4 * q + 4, :].bitcast(I32)
             )
+        x_word_tab = keep.tile([P, T], I32, name="x_word_tab")
+        d_word_tab = keep.tile([P, G], I32, name="d_word_tab")
+        d_rows = d_words[0].rearrange("p n t -> p (n t)").bitcast(I32)
+        for u in range(2):
+            cols = slice(G // 2 * u, G // 2 * (u + 1))
+            nc.sync.dma_start(d_word_tab[:, cols], d_rows[:, cols])
+        nc.sync.dma_start(x_word_tab[:], x_words[0].rearrange("p n t -> p (n t)").bitcast(I32))
+        tau_t = keep.tile([P, PACK], F32, name="tau_t")
+        nc.sync.dma_start(tau_t[:], tau.rearrange("(p b) o -> p (b o)", b=PACK))
         n1_t = load_list(n1, "n1_t")
         n2_t = load_list(n2, "n2_t")
+        gs_t = keep.tile([P, PACK], F32, name="gs_t")
+        nc.sync.dma_start(gs_t[:], gs.rearrange("(p t) o -> p (t o)", t=PACK))
         cand_t = load_list(cand, "cand_t")
         n3_t = load_list(n3, "n3_t")
-        tau_t = keep.tile([P, PACK], F32, name="tau_t")
-        nc.scalar.dma_start(tau_t[:], tau.rearrange("(p b) o -> p (b o)", b=PACK))
-        gs_t = keep.tile([P, PACK], F32, name="gs_t")
-        nc.scalar.dma_start(gs_t[:], gs.rearrange("(p t) o -> p (t o)", t=PACK))
 
-        s_win = [keep.tile([P, S_WIN], F32, name="s_win%d" % b) for b in range(C // P)]
+        s_win = {}
+
+        def open_window(b, tag):
+            s_win[b] = keep.tile([P, S_WIN], F32, name="s_win%d" % b, tag=tag)
+            nc.vector.memset(s_win[b][:, S:], 0.0)
+
+        for b in range(2):
+            open_window(b, "s_win%d" % b)
 
         d_bytes = keep.tile([P, H], U8, name="d_bytes", tag="d_bytes")
         nc.vector.tensor_copy(d_bytes[:], d_scale_tab[:].indirect(k1_t[:]))
@@ -81,12 +91,17 @@ def tile_picked_pqckgateegp_none_p_kernel(
 
         xq_plane = keep.tile([P, S], U8, name="xq_plane", align_bytes=64)
         nc.vector.tensor_copy(xq_plane[:], x_scale_tab[:].indirect(offs_t[:]))
-        xq_words = keep.tile([P, S], U32, name="xq_words", align_bytes=64)
-        nc.vector.tensor_copy(xq_words[:], x_word_tab[:].bitcast(U32).indirect(offs_t[:]))
         d_picked = keep.tile([P, H], U32, name="d_picked")
         nc.vector.tensor_copy(d_picked[:], d_word_tab[:].bitcast(U32).indirect(k1_t[:]))
         d_dealt = keep.tile([P, H], I32, name="d_dealt", align_bytes=64)
         deal(d_dealt[:], d_picked[:].bitcast(I32), 4)
+
+        xq_words = keep.tile([P, S], U32, name="xq_words", align_bytes=64)
+        for u in range(2):
+            nc.vector.tensor_copy(
+                xq_words[:, HALF * u : HALF * (u + 1)],
+                x_word_tab[:].bitcast(U32).indirect(offs_t[:, HALF // 16 * u : HALF // 16 * (u + 1)]),
+            )
 
         neg_tau = keep.tile([P, C // P], F32, name="neg_tau", tag="d_bytes")
         nc.scalar.activation(neg_tau[:], tau_t[:], ACT.Copy, scale=-1.0)
@@ -98,34 +113,39 @@ def tile_picked_pqckgateegp_none_p_kernel(
                 rhs=xq_words[:, cols].bitcast(FP8X4), rhs_scale=xq_plane[:, cols], start=True, stop=True,
             )
 
-        h0_ps = [psum.tile([P, HALF], F32, name="h0_ps%d" % u, tag="bank%d" % u) for u in range(2)]
-        for u in range(2):
-            first_product(h0_ps[u][:], 0, slice(HALF * u, HALF * (u + 1)))
         h_ps = {}
-        for t in range(1, PACK):
-            h_ps[t] = psum.tile([P, S], F32, name="h_ps%d" % t, tag="bank%d" % (t + 1))
+        for u in range(2):
+            for t in range(2):
+                h_ps[t, u] = psum.tile([P, HALF], F32, name="h_ps%d_%d" % (t, u), tag="bank%d" % (2 * t + u))
+                first_product(h_ps[t, u][:], t, slice(HALF * u, HALF * (u + 1)))
+        for t in range(2, PACK):
+            h_ps[t] = psum.tile([P, S], F32, name="h_ps%d" % t, tag="bank%d" % (t + 2))
             first_product(h_ps[t][:], t, slice(0, S))
 
-        h = [keep.tile([P, S], F32, name="h%d" % t) for t in range(PACK)]
-        old = [keep.tile([P, W], F32, name="old%d" % t) for t in range(PACK)]
-        pa = [keep.tile([P, W], F32, name="pa%d" % t) for t in range(PACK)]
-        th = [keep.tile([P, W], F32, name="th%d" % t) for t in range(PACK)]
-        ra = [keep.tile([P, W], F32, name="ra%d" % t) for t in range(PACK)]
+        h = {t: keep.tile([P, S], F32, name="h%d" % t) for t in range(2)}
+        for t in range(2):
+            nc.scalar.activation(h[t][:, :HALF], h_ps[t, 0][:], ACT.Copy, scale=0.0625)
+        ra = {}
         z = [keep.tile([P, HALF, PACK], BF16, name="z%d" % u, align_bytes=64) for u in range(2)]
 
         def fetch(t):
-            if t == 0:
-                nc.scalar.activation(h[0][:, :HALF], h0_ps[0][:], ACT.Copy, scale=0.0625)
-                nc.vector.tensor_scalar(h[0][:, HALF:], h0_ps[1][:], 0.0625, None, ALU.mult)
+            if t < 2:
+                nc.vector.tensor_scalar(h[t][:, HALF:], h_ps[t, 1][:], 0.0625, None, ALU.mult)
             else:
+                h[t] = keep.tile([P, S], F32, name="h%d" % t, tag="pa%d" % (t - 2))
                 nc.vector.tensor_scalar(h[t][:], h_ps[t][:], 0.0625, None, ALU.mult)
-            nc.scalar.activation(old[t][:], h[t][:].indirect(n1_t[:]), ACT.Copy, scale=0.5)
-            nc.vector.tensor_copy(pa[t][:], h[t][:].indirect(n2_t[:]))
-            nc.scalar.activation(th[t][:], pa[t][:], ACT.Tanh, scale=0.5)
-            nc.vector.scalar_tensor_tensor(ra[t][:], th[t][:], 1.0, old[t][:], ALU.add, ALU.mult)
+            upd = work.tile([P, 2, W], F32, name="upd", tag="upd")
+            pa = keep.tile([P, W], F32, name="pa%d" % t, tag="pa%d" % t)
+            nc.scalar.activation(upd[:, 0, :], h[t][:].indirect(n1_t[:]), ACT.Copy, scale=0.5)
+            nc.vector.tensor_copy(pa[:], h[t][:].indirect(n2_t[:]))
+            nc.scalar.activation(upd[:, 1, :], pa[:], ACT.Tanh, scale=0.5)
+            ra[t] = keep.tile([P, W], F32, name="ra%d" % t)
+            nc.vector.scalar_tensor_tensor(ra[t][:], upd[:, 1, :], 1.0, upd[:, 0, :], ALU.add, ALU.mult)
 
         def put(t):
             nc.scalar.activation(h[t][:].indirect(n1_t[:]), ra[t][:], ACT.Copy)
+
+        def weigh(t):
             for u in range(2):
                 nc.vector.tensor_scalar(
                     z[u][:, :, t], h[t][:, HALF * u : HALF * (u + 1)], gs_t[:, t : t + 1], None, ALU.mult
@@ -137,18 +157,24 @@ def tile_picked_pqckgateegp_none_p_kernel(
         fetch(2)
         put(1)
         fetch(3)
+        weigh(0)
 
-        xc_picked = keep.tile([P, C], U32, name="xc_picked")
+        xc_picked = keep.tile([P, C], U32, name="xc_picked", tag="pa2")
         nc.vector.tensor_copy(xc_picked[:], x_word_tab[:].bitcast(U32).indirect(cand_t[:]))
-        xc_bytes = keep.tile([P, C], U8, name="xc_bytes")
+        xc_bytes = keep.tile([P, C], U8, name="xc_bytes", tag="pa3")
         nc.vector.tensor_copy(xc_bytes[:], x_scale_tab[:].indirect(cand_t[:]))
         xc_words = keep.tile([P, C], I32, name="xc_words", align_bytes=64)
         deal(xc_words[:], xc_picked[:].bitcast(I32), 4)
         xc_plane = keep.tile([P, C], U8, name="xc_plane", align_bytes=64)
         deal(xc_plane[:], xc_bytes[:], 16)
 
+        weigh(1)
+        for b in range(2, PACK):
+            open_window(b, "pa%d" % b)
         put(2)
         put(3)
+        weigh(2)
+        weigh(3)
 
         z_words = keep.tile([P, S], U32, name="z_words", align_bytes=64)
         z_plane = keep.tile([P, S], U8, name="z_plane", align_bytes=64)
@@ -170,49 +196,69 @@ def tile_picked_pqckgateegp_none_p_kernel(
         tops = [keep.tile([P, 1], F32, name="top0_%d" % u) for u in range(2)]
         for u in range(2):
             cols = slice(HALF * u, HALF * (u + 1))
-            bank = psum.tile([P, HALF], F32, name="s_ps0_%d" % u, tag="bank%d" % (5 + u))
+            bank = psum.tile([P, HALF], F32, name="s_ps0_%d" % u, tag="bank%d" % (6 + u))
             score(bank[:], 0, cols)
             nc.vector.tensor_scalar(
                 s_win[0][:, cols], bank[:], 0.0625, tops[0][:] if u else None, ALU.mult, ALU.max, accum_out=tops[u][:]
             )
         nc.scalar.activation(bias[0][:], tops[1][:], ACT.Copy, scale=neg_tau[:, 0:1])
         for b in range(1, C // P):
-            bank = psum.tile([P, S], F32, name="s_ps%d" % b, tag="bank%d" % ((6 + b) % 8))
+            bank = psum.tile([P, S], F32, name="s_ps%d" % b, tag="bank%d" % (b - 1))
             score(bank[:], b, slice(0, S))
             top = keep.tile([P, 1], F32, name="top%d" % b)
             nc.vector.tensor_scalar(s_win[b][:, :S], bank[:], 0.0625, None, ALU.mult, ALU.max, accum_out=top[:])
             nc.vector.tensor_scalar(bias[b][:], top[:], neg_tau[:, b : b + 1], None, ALU.mult)
 
-        def exps(b, j0, n, hi, lo):
+        out_rows = out.rearrange("(p b) j -> p b j", b=PACK)
+
+        def exps(b, j0, n):
             ea = work.tile([P, n, MEMBERS], F32, name="ea", tag="ea", bufs=4)
             flat = ea[:].rearrange("p j m -> p (j m)")
-            for e0 in range(0, n * MEMBERS, EXP_N):
+            step = min(EXP_N, n * MEMBERS)
+            for e0 in range(0, n * MEMBERS, step):
                 c0 = (j0 * MEMBERS + e0) // 16
                 nc.scalar.activation(
-                    flat[:, e0 : e0 + EXP_N], s_win[b][:].indirect(n3_t[:, c0 : c0 + EXP_N // 16]), ACT.Exp,
+                    flat[:, e0 : e0 + step], s_win[b][:].indirect(n3_t[:, c0 : c0 + step // 16]), ACT.Exp,
                     bias=bias[b][:], scale=tau_t[:, b : b + 1],
                 )
-            nc.vector.tensor_tensor(hi[:, j0 : j0 + n, :], ea[:, :, 0:2], ea[:, :, 2:4], ALU.max)
-            nc.vector.tensor_tensor(lo[:, j0 : j0 + n, :], ea[:, :, 0:2], ea[:, :, 2:4], ALU.min)
+            return ea
 
-        def finish(b, j0, n, hi, lo):
-            cols = slice(j0, j0 + n)
+        def pair(dst, ea, j0, n, op):
+            nc.vector.tensor_tensor(dst[:, j0 : j0 + n, :], ea[:, :, 0:2], ea[:, :, 2:4], op)
+
+        def ends(hi, lo, j0, n):
             mx = work.tile([P, n], F32, name="mx", tag="mx")
             mn = work.tile([P, n], F32, name="mn", tag="mn")
-            nc.vector.tensor_tensor(mx[:], hi[:, cols, 0], hi[:, cols, 1], ALU.max)
-            nc.vector.tensor_tensor(mn[:], lo[:, cols, 0], lo[:, cols, 1], ALU.min)
+            nc.vector.tensor_tensor(mx[:], hi[:, j0 : j0 + n, 0], hi[:, j0 : j0 + n, 1], ALU.max)
+            nc.vector.tensor_tensor(mn[:], lo[:, j0 : j0 + n, 0], lo[:, j0 : j0 + n, 1], ALU.min)
+            return mx, mn
+
+        def spread(mx, mn, n):
             gap = work.tile([P, n], F32, name="gap", tag="gap")
             nc.vector.tensor_tensor(gap[:], mx[:], mn[:], ALU.subtract)
-            res = work.tile([P, n], F32, name="res", tag="res", bufs=3)
-            nc.vector.scalar_tensor_tensor(res[:], gap[:], 3.0, s_win[b][:, cols], ALU.mult, ALU.mult)
-            nc.sync.dma_start(out.rearrange("(p b) j -> p b j", b=PACK)[:, b, cols], res[:])
+            return gap
 
+        def store(b, gap, j0, n):
+            res = work.tile([P, n], F32, name="res", tag="res", bufs=3)
+            nc.vector.scalar_tensor_tensor(res[:], gap[:], 3.0, s_win[b][:, j0 : j0 + n], ALU.mult, ALU.mult)
+            nc.sync.dma_start(out_rows[:, b, j0 : j0 + n], res[:])
+
+        widths = [[128] * 4, [128] * 4, [256, 256], [256, 128, 128]]
+        waiting = None
         for b in range(C // P):
             hi = work.tile([P, S, 2], F32, name="hi", tag="hi")
             lo = work.tile([P, S, 2], F32, name="lo", tag="lo")
             j0 = 0
-            for n in ([128, 128, 256] if b == 0 else [256, 256]):
-                exps(b, j0, n, hi, lo)
+            for n in widths[b]:
+                ea = exps(b, j0, n)
+                pair(hi, ea, j0, n, ALU.max)
+                if waiting:
+                    gap = spread(waiting[2], waiting[3], HALF)
+                pair(lo, ea, j0, n, ALU.min)
+                if waiting:
+                    store(waiting[0], gap, waiting[1], HALF)
+                    waiting = None
                 j0 = j0 + n
                 if j0 % HALF == 0:
-                    finish(b, j0 - HALF, HALF, hi, lo)
+                    waiting = (b, j0 - HALF) + ends(hi, lo, j0 - HALF, HALF)
+        store(waiting[0], spread(waiting[2], waiting[3], HALF), waiting[1], HALF)

@@ -207,7 +207,7 @@ def tile_picked_pqckgateegp_none_p_kernel(
             score(bank[:], b, slice(0, S))
             top = keep.tile([P, 1], F32, name="top%d" % b)
             nc.vector.tensor_scalar(s_win[b][:, :S], bank[:], 0.0625, None, ALU.mult, ALU.max, accum_out=top[:])
-            nc.vector.tensor_scalar(bias[b][:], top[:], neg_tau[:, b : b + 1], None, ALU.mult)
+            nc.scalar.activation(bias[b][:], top[:], ACT.Copy, scale=neg_tau[:, b : b + 1])
 
         out_rows = out.rearrange("(p b) j -> p b j", b=PACK)
 
@@ -223,42 +223,36 @@ def tile_picked_pqckgateegp_none_p_kernel(
                 )
             return ea
 
-        def pair(dst, ea, j0, n, op):
-            nc.vector.tensor_tensor(dst[:, j0 : j0 + n, :], ea[:, :, 0:2], ea[:, :, 2:4], op)
-
-        def ends(hi, lo, j0, n):
-            mx = work.tile([P, n], F32, name="mx", tag="mx")
-            mn = work.tile([P, n], F32, name="mn", tag="mn")
-            nc.vector.tensor_tensor(mx[:], hi[:, j0 : j0 + n, 0], hi[:, j0 : j0 + n, 1], ALU.max)
-            nc.vector.tensor_tensor(mn[:], lo[:, j0 : j0 + n, 0], lo[:, j0 : j0 + n, 1], ALU.min)
-            return mx, mn
-
-        def spread(mx, mn, n):
-            gap = work.tile([P, n], F32, name="gap", tag="gap")
-            nc.vector.tensor_tensor(gap[:], mx[:], mn[:], ALU.subtract)
-            return gap
-
-        def store(b, gap, j0, n):
-            res = work.tile([P, n], F32, name="res", tag="res", bufs=3)
-            nc.vector.scalar_tensor_tensor(res[:], gap[:], 3.0, s_win[b][:, j0 : j0 + n], ALU.mult, ALU.mult)
-            nc.sync.dma_start(out_rows[:, b, j0 : j0 + n], res[:])
-
-        widths = [[128] * 4, [128] * 4, [256, 256], [256, 128, 128]]
-        waiting = None
+        last = C // P - 1
+        s3 = []
         for b in range(C // P):
-            hi = work.tile([P, S, 2], F32, name="hi", tag="hi")
-            lo = work.tile([P, S, 2], F32, name="lo", tag="lo")
-            j0 = 0
-            for n in widths[b]:
-                ea = exps(b, j0, n)
-                pair(hi, ea, j0, n, ALU.max)
-                if waiting:
-                    gap = spread(waiting[2], waiting[3], HALF)
-                pair(lo, ea, j0, n, ALU.min)
-                if waiting:
-                    store(waiting[0], gap, waiting[1], HALF)
-                    waiting = None
-                j0 = j0 + n
-                if j0 % HALF == 0:
-                    waiting = (b, j0 - HALF) + ends(hi, lo, j0 - HALF, HALF)
-        store(waiting[0], spread(waiting[2], waiting[3], HALF), waiting[1], HALF)
+            n = S if b < last else HALF
+            tripled = keep.tile([P, n], F32, name="s3_%d" % b)
+            nc.gpsimd.tensor_scalar(tripled[:], s_win[b][:, :n], 3.0, 0.0, ALU.mult, ALU.add)
+            s3.append(tripled)
+
+        for b in range(C // P):
+            for j0 in range(0, S, HALF):
+                cols = slice(j0, j0 + HALF)
+                final = (b, j0) == (last, HALF)
+                mx = work.tile([P, HALF], F32, name="mx", tag="mx", bufs=3)
+                mn = work.tile([P, HALF], F32, name="mn", tag="mn", bufs=3)
+                i0 = 0
+                for n in ([128, 64, 64] if final else [128, 128]):
+                    ea = exps(b, j0 + i0, n)
+                    nc.vector.tensor_reduce(mx[:, i0 : i0 + n], ea[:], mybir.AxisListType.X, ALU.max)
+                    nc.vector.tensor_reduce(mn[:, i0 : i0 + n], ea[:], mybir.AxisListType.X, ALU.min)
+                    i0 = i0 + n
+                gap = work.tile([P, HALF], F32, name="gap", tag="gap")
+                res = work.tile([P, HALF], F32, name="res", tag="res", bufs=3)
+                if not final:
+                    nc.gpsimd.tensor_tensor(gap[:], mx[:], mn[:], ALU.subtract)
+                    nc.gpsimd.tensor_tensor(res[:], gap[:], s3[b][:, cols], ALU.mult)
+                    nc.sync.dma_start(out_rows[:, b, cols], res[:])
+        quarters = [slice(0, HALF // 2), slice(HALF // 2, HALF)]
+        for part in quarters:
+            nc.vector.tensor_tensor(gap[:, part], mx[:, part], mn[:, part], ALU.subtract)
+        for part in quarters:
+            cols = slice(HALF + part.start, HALF + part.stop)
+            nc.vector.scalar_tensor_tensor(res[:, part], gap[:, part], 3.0, s_win[last][:, cols], ALU.mult, ALU.mult)
+            nc.sync.dma_start(out_rows[:, last, cols], res[:, part])

from contextlib import ExitStack

import concourse.mybir as mybir

K, T, S, G, H, W, C = 512, 1024, 512, 2048, 512, 384, 512
FLOPS = 2 * K * H * S + 2 * H * C * S

F32 = mybir.dt.float32
BF16 = mybir.dt.bfloat16
I32 = mybir.dt.int32
U32 = mybir.dt.uint32
U16 = mybir.dt.uint16
U8 = mybir.dt.uint8
FP8X4 = mybir.dt.float8_e4m3fn_x4
ALU = mybir.AluOpType
ACT = mybir.ActivationFunctionType

P = 128
PACK = 4
HALF = S // 2
MEMBERS = 4
S_WIN = 1024
EXP_N = 512


def tile_picked_pqckgateegp_none_p_kernel(
    tc, x_words, x_scales, d_words, d_scales, gs, tau, offs, k1, n1, n2, cand, n3, out
):
    nc = tc.nc
    with ExitStack() as ctx:
        keep = ctx.enter_context(tc.tile_pool(name="keep", bufs=1))
        work = ctx.enter_context(tc.tile_pool(name="work", bufs=2))
        psum = ctx.enter_context(tc.psum_pool(name="psum", bufs=1))

        def load_list(src, name):
            tile = keep.tile([P, src.shape[1]], U16, name=name)
            nc.sync.dma_start(tile[:], src)
            return tile

        def deal(dst, src, line):
            nc.vector.tensor_copy(
                dst.rearrange("p (t b i) -> p b t i", t=PACK, i=line),
                src.rearrange("p (b i t) -> p b t i", t=PACK, i=line),
            )

        d_scale_tab = keep.tile([P, G], U8, name="d_scale_tab")
        x_scale_tab = keep.tile([P, T], U8, name="x_scale_tab")
        d_plane = keep.tile([P, H], U8, name="d_plane", align_bytes=64)
        nc.vector.memset(d_scale_tab[:].bitcast(I32), 0)
        nc.vector.memset(x_scale_tab[:].bitcast(I32), 0)
        nc.vector.memset(d_plane[:].bitcast(I32), 0)

        k1_t = load_list(k1, "k1_t")
        nc.sync.dma_start(d_scale_tab[0:P:8, :].bitcast(I32), d_scales[0].bitcast(I32))
        offs_t = load_list(offs, "offs_t")
        for q in range(4):
            nc.sync.dma_start(
                x_scale_tab[32 * q : 32 * q + 4, :].bitcast(I32), x_scales[0, 4 * q : 4 * q + 4, :].bitcast(I32)
            )
        x_word_tab = keep.tile([P, T], I32, name="x_word_tab")
        d_word_tab = keep.tile([P, G], I32, name="d_word_tab")
        d_rows = d_words[0].rearrange("p n t -> p (n t)").bitcast(I32)
        for u in range(2):
            cols = slice(G // 2 * u, G // 2 * (u + 1))
            nc.sync.dma_start(d_word_tab[:, cols], d_rows[:, cols])
        nc.sync.dma_start(x_word_tab[:], x_words[0].rearrange("p n t -> p (n t)").bitcast(I32))
        tau_t = keep.tile([P, PACK], F32, name="tau_t")
        nc.sync.dma_start(tau_t[:], tau.rearrange("(p b) o -> p (b o)", b=PACK))
        n1_t = load_list(n1, "n1_t")
        n2_t = load_list(n2, "n2_t")
        gs_t = keep.tile([P, PACK], F32, name="gs_t")
        nc.sync.dma_start(gs_t[:], gs.rearrange("(p t) o -> p (t o)", t=PACK))
        cand_t = load_list(cand, "cand_t")
        n3_t = load_list(n3, "n3_t")

        s_win = {}

        def open_window(b, tag):
            s_win[b] = keep.tile([P, S_WIN], F32, name="s_win%d" % b, tag=tag)
            nc.vector.memset(s_win[b][:, S:], 0.0)

        for b in range(2):
            open_window(b, "s_win%d" % b)

        d_bytes = keep.tile([P, H], U8, name="d_bytes", tag="d_bytes")
        nc.vector.tensor_copy(d_bytes[:], d_scale_tab[:].indirect(k1_t[:]))
        d_dealt_bytes = keep.tile([P, H], U8, name="d_dealt_bytes")
        deal(d_dealt_bytes[:], d_bytes[:], 16)
        for r in range(4):
            nc.scalar.dma_start(d_plane[r:P:32, :].bitcast(I32), d_dealt_bytes[8 * r : P : 32, :].bitcast(I32))

        xq_plane = keep.tile([P, S], U8, name="xq_plane", align_bytes=64)
        nc.vector.tensor_copy(xq_plane[:], x_scale_tab[:].indirect(offs_t[:]))
        d_picked = keep.tile([P, H], U32, name="d_picked")
        nc.vector.tensor_copy(d_picked[:], d_word_tab[:].bitcast(U32).indirect(k1_t[:]))
        d_dealt = keep.tile([P, H], I32, name="d_dealt", align_bytes=64)
        deal(d_dealt[:], d_picked[:].bitcast(I32), 4)

        xq_words = keep.tile([P, S], U32, name="xq_words", align_bytes=64)
        for u in range(2):
            nc.vector.tensor_copy(
                xq_words[:, HALF * u : HALF * (u + 1)],
                x_word_tab[:].bitcast(U32).indirect(offs_t[:, HALF // 16 * u : HALF // 16 * (u + 1)]),
            )

        neg_tau = keep.tile([P, C // P], F32, name="neg_tau", tag="d_bytes")
        nc.scalar.activation(neg_tau[:], tau_t[:], ACT.Copy, scale=-1.0)

        def first_product(bank, t, cols):
            rows = slice(P * t, P * (t + 1))
            nc.tensor.matmul_mx(
                out=bank, lhsT=d_dealt[:, rows].bitcast(FP8X4), lhsT_scale=d_plane[:, rows],
                rhs=xq_words[:, cols].bitcast(FP8X4), rhs_scale=xq_plane[:, cols], start=True, stop=True,
            )

        h_ps = {}
        for u in range(2):
            for t in range(2):
                h_ps[t, u] = psum.tile([P, HALF], F32, name="h_ps%d_%d" % (t, u), tag="bank%d" % (2 * t + u))
                first_product(h_ps[t, u][:], t, slice(HALF * u, HALF * (u + 1)))
        for t in range(2, PACK):
            h_ps[t] = psum.tile([P, S], F32, name="h_ps%d" % t, tag="bank%d" % (t + 2))
            first_product(h_ps[t][:], t, slice(0, S))

        h = {t: keep.tile([P, S], F32, name="h%d" % t) for t in range(2)}
        for t in range(2):
            nc.scalar.activation(h[t][:, :HALF], h_ps[t, 0][:], ACT.Copy, scale=0.0625)
        ra = {}
        z = [keep.tile([P, HALF, PACK], BF16, name="z%d" % u, align_bytes=64) for u in range(2)]

        def fetch(t):
            if t < 2:
                nc.vector.tensor_scalar(h[t][:, HALF:], h_ps[t, 1][:], 0.0625, None, ALU.mult)
            else:
                h[t] = keep.tile([P, S], F32, name="h%d" % t, tag="pa%d" % (t - 2))
                nc.vector.tensor_scalar(h[t][:], h_ps[t][:], 0.0625, None, ALU.mult)
            upd = work.tile([P, 2, W], F32, name="upd", tag="upd")
            pa = keep.tile([P, W], F32, name="pa%d" % t, tag="pa%d" % t)
            nc.scalar.activation(upd[:, 0, :], h[t][:].indirect(n1_t[:]), ACT.Copy, scale=0.5)
            nc.vector.tensor_copy(pa[:], h[t][:].indirect(n2_t[:]))
            nc.scalar.activation(upd[:, 1, :], pa[:], ACT.Tanh, scale=0.5)
            ra[t] = keep.tile([P, W], F32, name="ra%d" % t)
            nc.vector.scalar_tensor_tensor(ra[t][:], upd[:, 1, :], 1.0, upd[:, 0, :], ALU.add, ALU.mult)

        def put(t):
            nc.scalar.activation(h[t][:].indirect(n1_t[:]), ra[t][:], ACT.Copy)

        def weigh(t):
            for u in range(2):
                nc.vector.tensor_scalar(
                    z[u][:, :, t], h[t][:, HALF * u : HALF * (u + 1)], gs_t[:, t : t + 1], None, ALU.mult
                )

        fetch(0)
        fetch(1)
        put(0)
        fetch(2)
        put(1)
        fetch(3)
        weigh(0)

        xc_picked = keep.tile([P, C], U32, name="xc_picked", tag="pa2")
        nc.vector.tensor_copy(xc_picked[:], x_word_tab[:].bitcast(U32).indirect(cand_t[:]))
        xc_bytes = keep.tile([P, C], U8, name="xc_bytes", tag="pa3")
        nc.vector.tensor_copy(xc_bytes[:], x_scale_tab[:].indirect(cand_t[:]))
        xc_words = keep.tile([P, C], I32, name="xc_words", align_bytes=64)
        deal(xc_words[:], xc_picked[:].bitcast(I32), 4)
        xc_plane = keep.tile([P, C], U8, name="xc_plane", align_bytes=64)
        deal(xc_plane[:], xc_bytes[:], 16)

        weigh(1)
        for b in range(2, PACK):
            open_window(b, "pa%d" % b)
        put(2)
        put(3)
        weigh(2)
        weigh(3)

        z_words = keep.tile([P, S], U32, name="z_words", align_bytes=64)
        z_plane = keep.tile([P, S], U8, name="z_plane", align_bytes=64)
        for u in range(2):
            cols = slice(HALF * u, HALF * (u + 1))
            nc.vector.quantize_mx(
                out=z_words[:, cols].bitcast(FP8X4), scales=z_plane[:, cols],
                in_=z[u][:].rearrange("p j t -> p (j t)"),
            )

        def score(bank, b, cols):
            rows = slice(P * b, P * (b + 1))
            nc.tensor.matmul_mx(
                out=bank, lhsT=xc_words[:, rows].bitcast(FP8X4), lhsT_scale=xc_plane[:, rows],
                rhs=z_words[:, cols].bitcast(FP8X4), rhs_scale=z_plane[:, cols], start=True, stop=True,
            )

        bias = [keep.tile([P, 1], F32, name="bias%d" % b) for b in range(C // P)]
        tops = [keep.tile([P, 1], F32, name="top0_%d" % u) for u in range(2)]
        for u in range(2):
            cols = slice(HALF * u, HALF * (u + 1))
            bank = psum.tile([P, HALF], F32, name="s_ps0_%d" % u, tag="bank%d" % (6 + u))
            score(bank[:], 0, cols)
            nc.vector.tensor_scalar(
                s_win[0][:, cols], bank[:], 0.0625, tops[0][:] if u else None, ALU.mult, ALU.max, accum_out=tops[u][:]
            )
        nc.scalar.activation(bias[0][:], tops[1][:], ACT.Copy, scale=neg_tau[:, 0:1])
        for b in range(1, C // P):
            bank = psum.tile([P, S], F32, name="s_ps%d" % b, tag="bank%d" % (b - 1))
            score(bank[:], b, slice(0, S))
            top = keep.tile([P, 1], F32, name="top%d" % b)
            nc.vector.tensor_scalar(s_win[b][:, :S], bank[:], 0.0625, None, ALU.mult, ALU.max, accum_out=top[:])
            nc.scalar.activation(bias[b][:], top[:], ACT.Copy, scale=neg_tau[:, b : b + 1])

        out_rows = out.rearrange("(p b) j -> p b j", b=PACK)

        def exps(b, j0, n):
            ea = work.tile([P, n, MEMBERS], F32, name="ea", tag="ea", bufs=4)
            flat = ea[:].rearrange("p j m -> p (j m)")
            step = min(EXP_N, n * MEMBERS)
            for e0 in range(0, n * MEMBERS, step):
                c0 = (j0 * MEMBERS + e0) // 16
                nc.scalar.activation(
                    flat[:, e0 : e0 + step], s_win[b][:].indirect(n3_t[:, c0 : c0 + step // 16]), ACT.Exp,
                    bias=bias[b][:], scale=tau_t[:, b : b + 1],
                )
            return ea

        last = C // P - 1
        s3 = []
        for b in range(C // P):
            n = S if b < last else HALF
            tripled = keep.tile([P, n], F32, name="s3_%d" % b)
            nc.gpsimd.tensor_scalar(tripled[:], s_win[b][:, :n], 3.0, 0.0, ALU.mult, ALU.add)
            s3.append(tripled)

        for b in range(C // P):
            for j0 in range(0, S, HALF):
                cols = slice(j0, j0 + HALF)
                final = (b, j0) == (last, HALF)
                mx = work.tile([P, HALF], F32, name="mx", tag="mx", bufs=3)
                mn = work.tile([P, HALF], F32, name="mn", tag="mn", bufs=3)
                i0 = 0
                for n in ([128, 64, 64] if final else [128, 128]):
                    ea = exps(b, j0 + i0, n)
                    nc.vector.tensor_reduce(mx[:, i0 : i0 + n], ea[:], mybir.AxisListType.X, ALU.max)
                    nc.vector.tensor_reduce(mn[:, i0 : i0 + n], ea[:], mybir.AxisListType.X, ALU.min)
                    i0 = i0 + n
                gap = work.tile([P, HALF], F32, name="gap", tag="gap")
                res = work.tile([P, HALF], F32, name="res", tag="res", bufs=3)
                if not final:
                    nc.gpsimd.tensor_tensor(gap[:], mx[:], mn[:], ALU.subtract)
                    nc.gpsimd.tensor_tensor(res[:], gap[:], s3[b][:, cols], ALU.mult)
                    nc.sync.dma_start(out_rows[:, b, cols], res[:])
        quarters = [slice(0, HALF // 2), slice(HALF // 2, HALF)]
        for part in quarters:
            nc.vector.tensor_tensor(gap[:, part], mx[:, part], mn[:, part], ALU.subtract)
        for part in quarters:
            cols = slice(HALF + part.start, HALF + part.stop)
            nc.vector.scalar_tensor_tensor(res[:, part], gap[:, part], 3.0, s_win[last][:, cols], ALU.mult, ALU.mult)
            nc.sync.dma_start(out_rows[:, last, cols], res[:, part])
